import numpy as np
import ml_dtypes


def mxq(x, axis, fmt="e4m3"):
    dtype, down = {"e4m3": (ml_dtypes.float8_e4m3fn, 7), "e5m2": (ml_dtypes.float8_e5m2, 14)}[fmt]
    v = np.moveaxis(np.asarray(x, np.float32).astype(ml_dtypes.bfloat16).astype(np.float64), axis, -1)
    blocks = v.reshape(v.shape[:-1] + (-1, 32))
    amax = np.abs(blocks).max(-1, keepdims=True)
    byte = np.maximum(np.where(amax > 0, np.frexp(amax)[1] - 1 + 127, 0) - down, 1)
    scale = np.exp2(byte - 127.0)
    codes = (blocks / scale).astype(np.float32).astype(dtype).astype(np.float64)
    return np.moveaxis((codes * scale).reshape(v.shape), -1, axis)


WIDE = False


def mx_kscale(k):
    if not WIDE:
        return np.ones(k)
    levels = np.array([10, -10, 5, -5, 0])
    if k % 512:
        return np.exp2(np.random.permutation(np.resize(levels, k // 32))).repeat(32)
    a = np.empty((k // 512, 16))
    for p in range(k // 512):
        a[p, :8] = np.random.permutation(np.resize(levels, 8))
        for g in range(8):
            far = levels[np.abs(levels - a[p, g]) >= 10]
            a[p, g + 8] = far[np.random.randint(len(far))]
    return np.exp2(a.ravel()).repeat(32)


def f64(x):
    return np.asarray(x).astype(np.float64)


def striped(idx):
    return np.tile(idx.reshape(-1, 16).T, (8, 1)).astype(np.uint16)


def unstriped(offs):
    return offs[:16].T.reshape(-1).astype(np.int64)


E2M1 = np.array([0.0, 0.5, 1.0, 1.5, 2.0, 3.0, 4.0, 6.0, -0.0, -0.5, -1.0, -1.5, -2.0, -3.0, -4.0, -6.0])


def pack_weight(w, fmt):
    k, n = w.shape
    w = f64(np.asarray(w, np.float32).astype(ml_dtypes.bfloat16)).reshape(k // 32, 32, n)
    amax = np.abs(w).max(1)
    if fmt == "e4m3":
        byte = np.frexp(amax)[1] - 1 + 127 - 7
    else:
        mant, ex = np.frexp(amax / 6.0)
        byte = np.where(mant > 0.5, ex, ex - 1) + 127
    byte = np.clip(np.where(amax > 0, byte, 1), 1, 254)
    scaled = (w * np.exp2(127.0 - byte)[:, None, :]).reshape(k, n).astype(np.float32)
    by_word = np.ascontiguousarray(scaled.reshape(k // 512, 128, 4, n).transpose(0, 1, 3, 2))
    if fmt == "e4m3":
        words = by_word.astype(ml_dtypes.float8_e4m3fn).view(np.uint8)
    else:
        c = by_word.astype(ml_dtypes.float4_e2m1fn).view(np.uint8) & 0xF
        words = (c[..., 0::2] | (c[..., 1::2] << 4)).reshape(k // 512, 128, 2 * n)
    return np.ascontiguousarray(words), np.ascontiguousarray(byte.astype(np.uint8).reshape(k // 512, 16, n))


def unpack_weight(words, scales, fmt):
    g, _, n = scales.shape
    words = np.ascontiguousarray(words).reshape(g, 128, n, -1)
    if fmt == "e4m3":
        vals = words.view(ml_dtypes.float8_e4m3fn).astype(np.float64)
    else:
        nib = np.empty((g, 128, n, 4), np.uint8)
        nib[..., 0::2] = words & 0xF
        nib[..., 1::2] = words >> 4
        vals = E2M1[nib]
    vals = vals * np.repeat(np.exp2(scales.astype(np.float64) - 127.0), 8, axis=1)[..., None]
    return vals.transpose(0, 1, 3, 2).reshape(g * 512, n)


def gelu(v):
    return 0.5 * v * (1.0 + np.tanh(np.sqrt(2.0 / np.pi) * (v + 0.044715 * v**3)))


def striped8(idx):
    return np.concatenate([v.reshape(-1, 16).T for v in idx]).astype(np.uint16)


def unstriped8(offs):
    return np.stack([offs[16 * g:16 * g + 16].T.reshape(-1) for g in range(8)]).astype(np.int64)


def runs(v, idx8):
    k = np.arange(v.shape[0])
    return v[k[:, None], idx8[k % 512 // 64]]


def bf(x):
    return np.asarray(x, np.float32).astype(ml_dtypes.bfloat16)


def planes(Y):
    n, m = Y.shape
    b = f64(bf(Y)).reshape(n // 32, 32, m)
    amax = np.abs(b).max(1)
    byte = np.clip(np.where(amax > 0, np.frexp(amax)[1] - 1 + 127 - 7, 1), 1, 254)
    codes = (b * np.exp2(127.0 - byte)[:, None, :]).reshape(n, m).astype(np.float32).astype(ml_dtypes.float8_e4m3fn).view(np.uint8)
    words = codes.reshape(n // 512, 128, 4, m).transpose(0, 1, 3, 2)
    return np.ascontiguousarray(words), np.ascontiguousarray(byte.astype(np.uint8).reshape(n // 512, 16, m))


K, T, S, P, H, N = 1536, 2048, 1024, 512, 1024, 512

def setup_inputs():
    n = np.random.standard_normal
    s = mx_kscale(K)[:, None]
    u = mx_kscale(H)[:, None]
    tab_words, tab_scales = pack_weight(n((K, T)) * s, "e4m3")
    w4 = n((H, N)) / np.sqrt(H) * np.exp(0.8 * n(N))[None, :] / u
    w4_words, w4_scales = pack_weight(w4, "e2m1")
    idx8 = np.stack([np.random.permutation(S)[:P] for _ in range(8)])
    return {
        "tab_words": tab_words,
        "tab_scales": tab_scales,
        "offs": striped(np.random.permutation(T)[:S]),
        "offs2": striped8(idx8),
        "w1": (0.7 * n((K, H)) / np.sqrt(K) / s).astype(np.float32),
        "hall": np.random.uniform(0.6, 1.4, (H, S)).astype(np.float32),
        "mark": (5.0 * n((H, P)) * u).astype(np.float32),
        "gain": (np.random.uniform(0.5, 1.5, H) * u[:, 0]).astype(np.float32),
        "w4_words": w4_words,
        "w4_scales": w4_scales,
    }

def reference(tab_words, tab_scales, offs, offs2, w1, hall, mark, gain, w4_words, w4_scales):
    v = unpack_weight(tab_words, tab_scales, "e4m3")[:, unstriped(offs)]
    h = f64(hall) * (mxq(f64(w1), 0, "e4m3").T @ v)
    top = h.max(axis=1)
    hp = runs(h, unstriped8(offs2))
    a = np.exp(hp - top[:, None])
    z = f64(mark) * a + f64(gain)[:, None] * hp
    w4 = unpack_weight(w4_words, w4_scales, "e2m1")
    y = w4.T @ mxq(z, 0, "e4m3")
    words, scales = planes(y)
    return y, words, scales

@@ -1,0 +1,318 @@
+from contextlib import ExitStack
+
+import concourse.mybir as mybir
+
+K, T, S, M, H, N = 1536, 2048, 1024, 512, 1024, 512
+FLOPS = 2 * K * H * S + 2 * H * N * M
+
+F32 = mybir.dt.float32
+BF16 = mybir.dt.bfloat16
+I32 = mybir.dt.int32
+U32 = mybir.dt.uint32
+U16 = mybir.dt.uint16
+U8 = mybir.dt.uint8
+E4M3 = mybir.dt.float8_e4m3fn_x4
+E2M1 = mybir.dt.float4_e2m1fn_x4
+ALU = mybir.AluOpType
+ACT = mybir.ActivationFunctionType
+AX = mybir.AxisListType
+
+P = 128
+BANK = 512
+HALF = 256
+
+
+def tile_list_ringing_evenness_kernel(
+    tc, tab_words, tab_scales, offs, offs2, w1, hall, mark, gain, w4_words, w4_scales, out_0, out_1, out_2
+):
+    nc = tc.nc
+    with ExitStack() as ctx:
+        keep = ctx.enter_context(tc.tile_pool(name="keep", bufs=1))
+        raws = ctx.enter_context(tc.tile_pool(name="raws", bufs=4))
+        casts = ctx.enter_context(tc.tile_pool(name="casts", bufs=4))
+        looks = ctx.enter_context(tc.tile_pool(name="looks", bufs=8))
+        hs = ctx.enter_context(tc.tile_pool(name="hs", bufs=8))
+        psum = ctx.enter_context(tc.psum_pool(name="psum", bufs=1))
+
+        offs_t = keep.tile([P, S // 16], U16, name="offs_t")
+        offs2_t = keep.tile([P, M // 16], U16, name="offs2_t")
+        tab_t = [keep.tile([P, T], U32, name="tab%d" % a) for a in range(3)]
+        tab_s = keep.tile([P, T], U8, name="tab_s")
+        v_words = [[keep.tile([P, BANK], U32, name="vw%d%d" % (a, c), align_bytes=64) for c in range(2)] for a in range(3)]
+        v_scales = [keep.tile([P, BANK], U8, name="vs%d" % c, align_bytes=64) for c in range(2)]
+        w1_codes = {}
+        w1_scales = {}
+        for b in range(2):
+            for a in range(3):
+                for u in range(2):
+                    w1_codes[b, a, u] = keep.tile([P, 2 * P], U32, name="w1c%d%d%d" % (b, a, u), align_bytes=64)
+                    w1_scales[b, a, u] = keep.tile([P, 2 * P], U8, name="w1s%d%d%d" % (b, a, u), align_bytes=64)
+        hall_t = [keep.tile([P, S], F32, name="hall%d" % n) for n in range(8)]
+        gain_t = keep.tile([P, 2, 4], F32, name="gain_t")
+        ntop = [keep.tile([P, 1], F32, name="ntop%d" % n) for n in range(8)]
+        w4_raw = keep.tile([P, 2, N], U16, name="w4_raw")
+        w4s_raw = keep.tile([P, 2 * N], U8, name="w4s_raw")
+        w4_t = keep.tile([P, 2 * N], U16, name="w4_t", align_bytes=64)
+        w4s_t = keep.tile([P, 2 * N], U8, name="w4s_t", align_bytes=64)
+        z_codes = [[keep.tile([P, HALF], U32, name="zc%d%d" % (b, c), align_bytes=64) for c in range(2)] for b in range(2)]
+        z_scales = [[keep.tile([P, HALF], U8, name="zs%d%d" % (b, c), align_bytes=64) for c in range(2)] for b in range(2)]
+        y_codes = keep.tile([P, M], U32, name="y_codes", align_bytes=64)
+        y_scales = keep.tile([P, M], U8, name="y_scales", align_bytes=64)
+
+        w1_raw = {}
+        w1_cast = {}
+        mark_t = {}
+        h_t = {}
+        a_t = {}
+        hp_t = {}
+        h_bank = {}
+        y_bank = {}
+        z_cast = {}
+
+        def load_tab(a):
+            nc.sync.dma_start(out=tab_t[a][:].bitcast(I32), in_=tab_words[a].rearrange("p t i -> p (t i)").bitcast(I32))
+
+        def load_w1(b, a):
+            w1_raw[b, a] = raws.tile([P, 4, BANK], F32, name="raw", tag="raw")
+            nc.sync.dma_start(
+                out=w1_raw[b, a][:],
+                in_=w1[512 * a : 512 * (a + 1), 512 * b : 512 * (b + 1)].rearrange("(p j) c -> p j c", j=4),
+            )
+
+        def load_hall(n):
+            b, i = divmod(n, 4)
+            nc.sync.dma_start(
+                out=hall_t[n][:], in_=hall[512 * b : 512 * (b + 1), :].rearrange("(p i) s -> p i s", i=4)[:, i, :]
+            )
+
+        def load_mark(b):
+            mark_t[b] = raws.tile([P, 4, M], F32, name="raw", tag="raw")
+            nc.sync.dma_start(out=mark_t[b][:], in_=mark[512 * b : 512 * (b + 1), :].rearrange("(p i) m -> p i m", i=4))
+
+        def load_w4():
+            nc.sync.dma_start(out=w4_raw[:].bitcast(I32), in_=w4_words.bitcast(I32).rearrange("a p c -> p a c"))
+            for q in range(4):
+                nc.sync.dma_start(
+                    out=w4s_raw[32 * q : 32 * q + 4, :].bitcast(I32).rearrange("r (a c) -> r a c", a=2),
+                    in_=w4_scales[:, 4 * q : 4 * q + 4, :].bitcast(I32).rearrange("a r c -> r a c"),
+                )
+
+        def deal_w4():
+            nc.scalar.copy(
+                out=w4_t[:].rearrange("p (a t q) -> p a t q", a=2, t=4),
+                in_=w4_raw[:].rearrange("p a (q t) -> p a t q", t=4),
+            )
+            nc.vector.tensor_copy(
+                out=w4s_t[:].rearrange("p (a t q) -> p a t q", a=2, t=4),
+                in_=w4s_raw[:].rearrange("p (a q t) -> p a t q", a=2, t=4),
+            )
+
+        def gather_words(a, c):
+            nc.vector.tensor_copy(out=v_words[a][c][:], in_=tab_t[a][:].indirect(offs_t[:, 32 * c : 32 * (c + 1)]))
+
+        def gather_scales(c):
+            nc.vector.tensor_copy(out=v_scales[c][:], in_=tab_s[:].indirect(offs_t[:, 32 * c : 32 * (c + 1)]))
+
+        def cast_w1(b, a, u, eng):
+            w1_cast[b, a, u] = casts.tile([P, 2 * P * 4], BF16, name="cast", tag="cast", align_bytes=64)
+            dst = w1_cast[b, a, u][:].rearrange("p (t m j) -> p m j t", t=2, j=4)
+            src = w1_raw[b, a][:].rearrange("p j (m t) -> p m j t", t=4)[:, :, :, 2 * u : 2 * u + 2]
+            if eng == "v":
+                nc.vector.tensor_copy(out=dst, in_=src)
+            elif eng == "s":
+                nc.scalar.activation(out=dst, in_=src, func=ACT.Copy)
+            else:
+                nc.gpsimd.tensor_scalar(out=dst, in0=src, scalar1=1.0, scalar2=0.0, op0=ALU.mult, op1=ALU.add)
+
+        def quant_w1(b, a, u):
+            nc.vector.quantize_mx(
+                out=w1_codes[b, a, u][:].bitcast(E4M3), scales=w1_scales[b, a, u][:], in_=w1_cast[b, a, u][:]
+            )
+
+        def mm1(n, a, c):
+            b, i = divmod(n, 4)
+            if a == 0:
+                h_bank[n, c] = psum.tile([P, BANK], F32, name="bank", tag="bank%d" % (2 * i + c))
+            cols = slice(P * (i % 2), P * (i % 2 + 1))
+            nc.tensor.matmul_mx(
+                out=h_bank[n, c][:],
+                lhsT=w1_codes[b, a, i // 2][:, cols].bitcast(E4M3),
+                lhsT_scale=w1_scales[b, a, i // 2][:, cols],
+                rhs=v_words[a][c][:].bitcast(E4M3),
+                rhs_scale=v_scales[c][4 * a : P, :],
+                start=(a == 0),
+                stop=(a == 2),
+            )
+
+        def make_h(n):
+            h_t[n] = hs.tile([P, S], F32, name="h", tag="h")
+            for c in range(2):
+                cols = slice(BANK * c, BANK * (c + 1))
+                nc.vector.tensor_tensor(out=h_t[n][:, cols], in0=h_bank[n, c][:], in1=hall_t[n][:, cols], op=ALU.mult)
+            nc.vector.reduce_max(out=ntop[n][:], in_=h_t[n][:], axis=AX.X, negate=True)
+
+        def alloc_looks(n):
+            a_t[n] = looks.tile([P, M], F32, name="a", tag="a")
+            hp_t[n] = looks.tile([P, M], F32, name="hp", tag="hp")
+
+        def look_copy(n, m0, m1):
+            nc.scalar.activation(out=hp_t[n][:, m0:m1], in_=h_t[n][:].indirect(offs2_t[:, m0 // 16 : m1 // 16]), func=ACT.Copy)
+
+        def look_exp(n, m0, m1):
+            nc.scalar.activation(
+                out=a_t[n][:, m0:m1], in_=h_t[n][:].indirect(offs2_t[:, m0 // 16 : m1 // 16]), func=ACT.Exp, bias=ntop[n][:]
+            )
+
+        def marked(n, m0, m1, eng):
+            b, i = divmod(n, 4)
+            rows = mark_t[b][:, i, m0:m1]
+            if eng == "v":
+                nc.vector.tensor_tensor(out=rows, in0=rows, in1=a_t[n][:, m0:m1], op=ALU.mult)
+            else:
+                nc.gpsimd.tensor_tensor(out=rows, in0=rows, in1=a_t[n][:, m0:m1], op=ALU.mult)
+
+        def make_z(n, m0, m1):
+            b, i = divmod(n, 4)
+            rows = mark_t[b][:, i, m0:m1]
+            nc.vector.scalar_tensor_tensor(
+                out=rows, in0=hp_t[n][:, m0:m1], scalar=gain_t[:, b, i : i + 1], in1=rows, op0=ALU.mult, op1=ALU.add
+            )
+
+        def weave(dst_tile, src, eng):
+            dst = dst_tile[:].rearrange("p (c i t) -> p c t i", i=4, t=4)
+            src = src.rearrange("p t (c i) -> p c t i", i=4)
+            if eng == "v":
+                nc.vector.tensor_copy(out=dst, in_=src)
+            else:
+                nc.scalar.activation(out=dst, in_=src, func=ACT.Copy)
+
+        def cast_z(b, c, eng):
+            z_cast[b, c] = casts.tile([P, 4 * HALF], BF16, name="cast", tag="cast", align_bytes=64)
+            weave(z_cast[b, c], mark_t[b][:, :, HALF * c : HALF * (c + 1)], eng)
+
+        def quant_z(b, c):
+            nc.vector.quantize_mx(out=z_codes[b][c][:].bitcast(E4M3), scales=z_scales[b][c][:], in_=z_cast[b, c][:])
+
+        def mm2(b, t, c):
+            if b == 0:
+                y_bank[t, c] = psum.tile([P, HALF], F32, name="bank", tag="bank%d" % (2 * t + c))
+            cols = slice(N * b + P * t, N * b + P * (t + 1))
+            nc.tensor.matmul_mx(
+                out=y_bank[t, c][:],
+                lhsT=w4_t[:, cols].bitcast(E2M1),
+                lhsT_scale=w4s_t[:, cols],
+                rhs=z_codes[b][c][:].bitcast(E4M3),
+                rhs_scale=z_scales[b][c][:],
+                start=(b == 0),
+                stop=(b == 1),
+            )
+
+        def finish(c, y_all):
+            cols = slice(HALF * c, HALF * (c + 1))
+            y = y_all[:, c]
+            for t in range(4):
+                if t % 2 == 0:
+                    nc.vector.tensor_copy(out=y[:, t, :], in_=y_bank[t, c][:])
+                else:
+                    nc.scalar.copy(out=y[:, t, :], in_=y_bank[t, c][:])
+            nc.sync.dma_start(out=out_0.rearrange("(p t) m -> p t m", t=4)[:, :, cols], in_=y)
+            y_cast = casts.tile([P, 4 * HALF], BF16, name="cast", tag="cast", align_bytes=64)
+            weave(y_cast, y, "v")
+            nc.vector.quantize_mx(out=y_codes[:, cols].bitcast(E4M3), scales=y_scales[:, cols], in_=y_cast[:])
+            nc.sync.dma_start(
+                out=out_1[0].rearrange("p m t -> p (m t)").bitcast(I32)[:, cols], in_=y_codes[:, cols].bitcast(I32)
+            )
+
+        nc.vector.memset(tab_s[:].bitcast(I32), 0)
+        nc.gpsimd.memset(w4s_raw[:].bitcast(I32), 0)
+        load_tab(0)
+        nc.sync.dma_start(out=offs_t[:], in_=offs)
+        for q in range(4):
+            nc.scalar.dma_start(
+                out=tab_s[32 * q : 32 * q + 12, :].bitcast(I32), in_=tab_scales[:, 4 * q : 4 * q + 4, :].bitcast(I32)
+            )
+        load_w1(0, 0)
+        load_tab(1)
+        load_w1(0, 1)
+        load_tab(2)
+        load_w1(0, 2)
+        load_hall(0)
+        nc.sync.dma_start(out=offs2_t[:], in_=offs2)
+        nc.sync.dma_start(out=gain_t[:], in_=gain.rearrange("(b p i) -> p b i", b=2, i=4))
+        load_hall(1)
+        load_w1(1, 0)
+        for a in range(3):
+            for c in range(2):
+                gather_words(a, c)
+            if a == 0:
+                for c in range(2):
+                    gather_scales(c)
+            cast_w1(0, a, 0, "v" if a == 2 else "s")
+            cast_w1(0, a, 1, "s")
+            for u in range(2):
+                quant_w1(0, a, u)
+                for i in range(2):
+                    for c in range(2):
+                        mm1(2 * u + i, a, c)
+        load_hall(2)
+        load_w1(1, 1)
+        load_hall(3)
+        load_mark(0)
+        load_w1(1, 2)
+        load_hall(4)
+        load_w4()
+        load_hall(5)
+        load_hall(6)
+        load_hall(7)
+        load_mark(1)
+        for n in range(8):
+            if n >= 4:
+                for a in range(3):
+                    for c in range(2):
+                        mm1(n, a, c)
+            make_h(n)
+            alloc_looks(n)
+            if n < 7:
+                look_copy(n, 0, M)
+                look_exp(n, 0, M)
+            else:
+                for c in range(2):
+                    look_copy(n, HALF * c, HALF * (c + 1))
+                for c in range(2):
+                    look_exp(n, HALF * c, HALF * (c + 1))
+            if 1 <= n <= 3:
+                for u in range(2):
+                    cast_w1(1, n - 1, u, "s")
+                for u in range(2):
+                    quant_w1(1, n - 1, u)
+            if n >= 2:
+                marked(n - 2, 0, M, "v")
+                make_z(n - 2, 0, M)
+            if n == 5:
+                deal_w4()
+                for c in range(2):
+                    cast_z(0, c, "s")
+            if n == 6:
+                for c in range(2):
+                    quant_z(0, c)
+        for c in range(2):
+            for t in range(4):
+                mm2(0, t, c)
+        marked(6, 0, M, "v")
+        make_z(6, 0, M)
+        for c in range(2):
+            marked(7, HALF * c, HALF * (c + 1), "v")
+            make_z(7, HALF * c, HALF * (c + 1))
+            cast_z(1, c, "v" if c == 0 else "s")
+            quant_z(1, c)
+
+        y_all = raws.tile([P, 2, 4, HALF], F32, name="raw", tag="raw")
+        for c in range(2):
+            for t in range(4):
+                mm2(1, t, c)
+            finish(c, y_all)
+        for q in range(4):
+            queue = nc.sync if q % 2 == 0 else nc.scalar
+            queue.dma_start(
+                out=out_2[0, 4 * q : 4 * q + 4, :].bitcast(I32), in_=y_scales[32 * q : 32 * q + 4, :].bitcast(I32)
+            )

@@ -85,23 +85,31 @@ def tile_list_ringing_evenness_kernel(
                 out=hall_t[n][:], in_=hall[512 * b : 512 * (b + 1), :].rearrange("(p i) s -> p i s", i=4)[:, i, :]
             )
 
-        def load_mark(b):
-            mark_t[b] = raws.tile([P, 4, M], F32, name="raw", tag="raw")
-            nc.sync.dma_start(out=mark_t[b][:], in_=mark[512 * b : 512 * (b + 1), :].rearrange("(p i) m -> p i m", i=4))
+        def load_mark(n):
+            b, i = divmod(n, 4)
+            if i == 0:
+                mark_t[b] = raws.tile([P, 4, M], F32, name="raw", tag="raw")
+            nc.sync.dma_start(
+                out=mark_t[b][:, i, :], in_=mark[512 * b : 512 * (b + 1), :].rearrange("(p i) m -> p i m", i=4)[:, i, :]
+            )
 
-        def load_w4():
+        def load_w4_words():
             nc.sync.dma_start(out=w4_raw[:].bitcast(I32), in_=w4_words.bitcast(I32).rearrange("a p c -> p a c"))
+
+        def load_w4_scales():
             for q in range(4):
                 nc.sync.dma_start(
                     out=w4s_raw[32 * q : 32 * q + 4, :].bitcast(I32).rearrange("r (a c) -> r a c", a=2),
                     in_=w4_scales[:, 4 * q : 4 * q + 4, :].bitcast(I32).rearrange("a r c -> r a c"),
                 )
 
-        def deal_w4():
+        def deal_w4_words():
             nc.scalar.copy(
                 out=w4_t[:].rearrange("p (a t q) -> p a t q", a=2, t=4),
                 in_=w4_raw[:].rearrange("p a (q t) -> p a t q", t=4),
             )
+
+        def deal_w4_scales():
             nc.vector.tensor_copy(
                 out=w4s_t[:].rearrange("p (a t q) -> p a t q", a=2, t=4),
                 in_=w4s_raw[:].rearrange("p (a q t) -> p a t q", a=2, t=4),
@@ -223,15 +231,15 @@ def tile_list_ringing_evenness_kernel(
                 out=out_1[0].rearrange("p m t -> p (m t)").bitcast(I32)[:, cols], in_=y_codes[:, cols].bitcast(I32)
             )
 
-        nc.vector.memset(tab_s[:].bitcast(I32), 0)
+        nc.gpsimd.memset(tab_s[:].bitcast(I32), 0)
         nc.gpsimd.memset(w4s_raw[:].bitcast(I32), 0)
         load_tab(0)
         nc.sync.dma_start(out=offs_t[:], in_=offs)
+        load_w1(0, 0)
         for q in range(4):
-            nc.scalar.dma_start(
+            nc.sync.dma_start(
                 out=tab_s[32 * q : 32 * q + 12, :].bitcast(I32), in_=tab_scales[:, 4 * q : 4 * q + 4, :].bitcast(I32)
             )
-        load_w1(0, 0)
         load_tab(1)
         load_w1(0, 1)
         load_tab(2)
@@ -239,6 +247,7 @@ def tile_list_ringing_evenness_kernel(
         load_hall(0)
         nc.sync.dma_start(out=offs2_t[:], in_=offs2)
         nc.sync.dma_start(out=gain_t[:], in_=gain.rearrange("(b p i) -> p b i", b=2, i=4))
+        load_w4_words()
         load_hall(1)
         load_w1(1, 0)
         for a in range(3):
@@ -254,17 +263,25 @@ def tile_list_ringing_evenness_kernel(
                 for i in range(2):
                     for c in range(2):
                         mm1(2 * u + i, a, c)
+        deal_w4_words()
+        load_mark(0)
         load_hall(2)
+        load_mark(1)
         load_w1(1, 1)
         load_hall(3)
-        load_mark(0)
+        load_mark(2)
         load_w1(1, 2)
+        load_mark(3)
         load_hall(4)
-        load_w4()
         load_hall(5)
+        load_mark(4)
         load_hall(6)
+        load_mark(5)
         load_hall(7)
-        load_mark(1)
+        load_mark(6)
+        load_mark(7)
+        load_w4_scales()
+        cast_engine = "vsvsvs"
         for n in range(8):
             if n >= 4:
                 for a in range(3):
@@ -275,6 +292,7 @@ def tile_list_ringing_evenness_kernel(
             if n < 7:
                 look_copy(n, 0, M)
                 look_exp(n, 0, M)
+                marked(n, 0, M, "g")
             else:
                 for c in range(2):
                     look_copy(n, HALF * c, HALF * (c + 1))
@@ -282,30 +300,30 @@ def tile_list_ringing_evenness_kernel(
                     look_exp(n, HALF * c, HALF * (c + 1))
             if 1 <= n <= 3:
                 for u in range(2):
-                    cast_w1(1, n - 1, u, "s")
-                for u in range(2):
-                    quant_w1(1, n - 1, u)
-            if n >= 2:
-                marked(n - 2, 0, M, "v")
-                make_z(n - 2, 0, M)
-            if n == 5:
-                deal_w4()
+                    cast_w1(1, n - 1, u, cast_engine[2 * (n - 1) + u])
+            if n >= 3:
+                make_z(n - 3, 0, M)
+            if 1 <= n <= 3:
+                quant_w1(1, n - 1, 0)
+            if 2 <= n <= 4:
+                quant_w1(1, n - 2, 1)
+            if n == 6:
                 for c in range(2):
                     cast_z(0, c, "s")
-            if n == 6:
+            if n == 7:
+                deal_w4_scales()
                 for c in range(2):
                     quant_z(0, c)
         for c in range(2):
             for t in range(4):
                 mm2(0, t, c)
-        marked(6, 0, M, "v")
-        make_z(6, 0, M)
+        for n in range(8 - 3, 7):
+            make_z(n, 0, M)
         for c in range(2):
             marked(7, HALF * c, HALF * (c + 1), "v")
             make_z(7, HALF * c, HALF * (c + 1))
             cast_z(1, c, "v" if c == 0 else "s")
             quant_z(1, c)
-
         y_all = raws.tile([P, 2, 4, HALF], F32, name="raw", tag="raw")
         for c in range(2):
             for t in range(4):

@@ -28,10 +28,8 @@ def tile_list_ringing_evenness_kernel(
     nc = tc.nc
     with ExitStack() as ctx:
         keep = ctx.enter_context(tc.tile_pool(name="keep", bufs=1))
-        raws = ctx.enter_context(tc.tile_pool(name="raws", bufs=4))
-        casts = ctx.enter_context(tc.tile_pool(name="casts", bufs=4))
-        looks = ctx.enter_context(tc.tile_pool(name="looks", bufs=8))
-        hs = ctx.enter_context(tc.tile_pool(name="hs", bufs=8))
+        casts = ctx.enter_context(tc.tile_pool(name="casts", bufs=6))
+        hs = ctx.enter_context(tc.tile_pool(name="hs", bufs=6))
         psum = ctx.enter_context(tc.psum_pool(name="psum", bufs=1))
 
         offs_t = keep.tile([P, S // 16], U16, name="offs_t")
@@ -42,14 +40,10 @@ def tile_list_ringing_evenness_kernel(
         v_scales = [keep.tile([P, BANK], U8, name="vs%d" % c, align_bytes=64) for c in range(2)]
         w1_codes = {}
         w1_scales = {}
-        for b in range(2):
-            for a in range(3):
-                for u in range(2):
-                    w1_codes[b, a, u] = keep.tile([P, 2 * P], U32, name="w1c%d%d%d" % (b, a, u), align_bytes=64)
-                    w1_scales[b, a, u] = keep.tile([P, 2 * P], U8, name="w1s%d%d%d" % (b, a, u), align_bytes=64)
-        hall_t = [keep.tile([P, S], F32, name="hall%d" % n) for n in range(8)]
-        gain_t = keep.tile([P, 2, 4], F32, name="gain_t")
+        hall_t = [keep.tile([P, S], F32, name="hall%d" % n, tag="hall%d" % n, align_bytes=64) for n in range(8)]
+        gain_col = {}
         ntop = [keep.tile([P, 1], F32, name="ntop%d" % n) for n in range(8)]
+        top = [keep.tile([P, 1], F32, name="top%d" % n) for n in range(8)]
         w4_raw = keep.tile([P, 2, N], U16, name="w4_raw")
         w4s_raw = keep.tile([P, 2 * N], U8, name="w4s_raw")
         w4_t = keep.tile([P, 2 * N], U16, name="w4_t", align_bytes=64)
@@ -68,12 +62,13 @@ def tile_list_ringing_evenness_kernel(
         h_bank = {}
         y_bank = {}
         z_cast = {}
+        t_t = {}
 
         def load_tab(a):
             nc.sync.dma_start(out=tab_t[a][:].bitcast(I32), in_=tab_words[a].rearrange("p t i -> p (t i)").bitcast(I32))
 
         def load_w1(b, a):
-            w1_raw[b, a] = raws.tile([P, 4, BANK], F32, name="raw", tag="raw")
+            w1_raw[b, a] = keep.tile([P, 4, BANK], F32, name="raw", tag="raw%d" % ((3 * b + a) % 4), align_bytes=64)
             nc.sync.dma_start(
                 out=w1_raw[b, a][:],
                 in_=w1[512 * a : 512 * (a + 1), 512 * b : 512 * (b + 1)].rearrange("(p j) c -> p j c", j=4),
@@ -85,10 +80,14 @@ def tile_list_ringing_evenness_kernel(
                 out=hall_t[n][:], in_=hall[512 * b : 512 * (b + 1), :].rearrange("(p i) s -> p i s", i=4)[:, i, :]
             )
 
+        def load_marks(b):
+            mark_t[b] = keep.tile([P, 4, M], F32, name="raw", tag=["raw2","raw3"][b], align_bytes=64)
+            nc.sync.dma_start(out=mark_t[b][:], in_=mark[512 * b : 512 * (b + 1), :].rearrange("(p i) m -> p i m", i=4))
+
         def load_mark(n):
             b, i = divmod(n, 4)
             if i == 0:
-                mark_t[b] = raws.tile([P, 4, M], F32, name="raw", tag="raw")
+                mark_t[b] = keep.tile([P, 4, M], F32, name="raw", tag=["raw2","raw3"][b], align_bytes=64)
             nc.sync.dma_start(
                 out=mark_t[b][:, i, :], in_=mark[512 * b : 512 * (b + 1), :].rearrange("(p i) m -> p i m", i=4)[:, i, :]
             )
@@ -121,21 +120,44 @@ def tile_list_ringing_evenness_kernel(
         def gather_scales(c):
             nc.vector.tensor_copy(out=v_scales[c][:], in_=tab_s[:].indirect(offs_t[:, 32 * c : 32 * (c + 1)]))
 
-        def cast_w1(b, a, u, eng):
-            w1_cast[b, a, u] = casts.tile([P, 2 * P * 4], BF16, name="cast", tag="cast", align_bytes=64)
-            dst = w1_cast[b, a, u][:].rearrange("p (t m j) -> p m j t", t=2, j=4)
+        def cast_w1(b, a, u, eng, joint):
+            if not joint:
+                w1_cast[b, a, u] = casts.tile([P, 1024], BF16, name="cast", tag="cast", align_bytes=64)[:]
+            elif u == 0:
+                both = casts.tile([P, 2048], BF16, name="cast2", tag="cast2", bufs=2, align_bytes=64)
+                w1_cast[b, a] = both[:]
+                w1_cast[b, a, 0] = both[:, 0:1024]
+                w1_cast[b, a, 1] = both[:, 1024:2048]
+            dst = w1_cast[b, a, u].rearrange("p (t m j) -> p m j t", t=2, j=4)
             src = w1_raw[b, a][:].rearrange("p j (m t) -> p m j t", t=4)[:, :, :, 2 * u : 2 * u + 2]
             if eng == "v":
                 nc.vector.tensor_copy(out=dst, in_=src)
             elif eng == "s":
                 nc.scalar.activation(out=dst, in_=src, func=ACT.Copy)
             else:
-                nc.gpsimd.tensor_scalar(out=dst, in0=src, scalar1=1.0, scalar2=0.0, op0=ALU.mult, op1=ALU.add)
+                nc.gpsimd.tensor_scalar(
+                    out=w1_cast[b, a, u].rearrange("p (t m j) -> p m t j", t=2, j=4),
+                    in0=w1_raw[b, a][:].rearrange("p j (m t) -> p m t j", t=4)[:, :, 2 * u : 2 * u + 2, :],
+                    scalar1=1.0,
+                    scalar2=0.0,
+                    op0=ALU.mult,
+                    op1=ALU.add,
+                )
 
-        def quant_w1(b, a, u):
-            nc.vector.quantize_mx(
-                out=w1_codes[b, a, u][:].bitcast(E4M3), scales=w1_scales[b, a, u][:], in_=w1_cast[b, a, u][:]
-            )
+        def quant_w1(b, a, u, tag):
+            width = BANK if u is None else HALF
+            codes = keep.tile([P, width], U32, name="codes", tag=tag, align_bytes=64)
+            scales = keep.tile([P, width], U8, name="scales", tag="s" + tag, align_bytes=64)
+            if u is None:
+                for k in range(2):
+                    w1_codes[b, a, k] = codes[:, HALF * k : HALF * (k + 1)]
+                    w1_scales[b, a, k] = scales[:, HALF * k : HALF * (k + 1)]
+                rounded = w1_cast[b, a]
+            else:
+                w1_codes[b, a, u] = codes[:]
+                w1_scales[b, a, u] = scales[:]
+                rounded = w1_cast[b, a, u]
+            nc.vector.quantize_mx(out=codes[:].bitcast(E4M3), scales=scales[:], in_=rounded)
 
         def mm1(n, a, c):
             b, i = divmod(n, 4)
@@ -152,16 +174,27 @@ def tile_list_ringing_evenness_kernel(
                 stop=(a == 2),
             )
 
+        def load_gain_late():
+            late = keep.tile([P, 2, 4], F32, name="gain_late", tag="hall5", align_bytes=64)
+            nc.sync.dma_start(out=late[:], in_=gain.rearrange("(b p i) -> p b i", b=2, i=4))
+            for n in range(8):
+                gain_col[n] = late[:, n // 4, n % 4 : n % 4 + 1]
+
         def make_h(n):
-            h_t[n] = hs.tile([P, S], F32, name="h", tag="h")
             for c in range(2):
                 cols = slice(BANK * c, BANK * (c + 1))
-                nc.vector.tensor_tensor(out=h_t[n][:, cols], in0=h_bank[n, c][:], in1=hall_t[n][:, cols], op=ALU.mult)
-            nc.vector.reduce_max(out=ntop[n][:], in_=h_t[n][:], axis=AX.X, negate=True)
+                nc.vector.tensor_tensor(out=hall_t[n][:, cols], in0=h_bank[n, c][:], in1=hall_t[n][:, cols], op=ALU.mult)
+
+        def make_top(n):
+            h_t[n] = hs.tile([P, S], F32, name="h", tag="h")
+            nc.vector.tensor_scalar(
+                out=h_t[n][:], in0=hall_t[n][:], scalar1=1.0, scalar2=None, op0=ALU.mult, op1=ALU.max, accum_out=top[n][:]
+            )
+            nc.scalar.activation(out=ntop[n][:], in_=top[n][:], func=ACT.Copy, scale=-1.0)
 
         def alloc_looks(n):
-            a_t[n] = looks.tile([P, M], F32, name="a", tag="a")
-            hp_t[n] = looks.tile([P, M], F32, name="hp", tag="hp")
+            a_t[n] = keep.tile([P, M], F32, name="a", tag="a%d" % n, align_bytes=64)[:]
+            hp_t[n] = keep.tile([P, M], F32, name="hp", tag="hp%d" % n, align_bytes=64)[:]
 
         def look_copy(n, m0, m1):
             nc.scalar.activation(out=hp_t[n][:, m0:m1], in_=h_t[n][:].indirect(offs2_t[:, m0 // 16 : m1 // 16]), func=ACT.Copy)
@@ -173,17 +206,19 @@ def tile_list_ringing_evenness_kernel(
 
         def marked(n, m0, m1, eng):
             b, i = divmod(n, 4)
-            rows = mark_t[b][:, i, m0:m1]
-            if eng == "v":
-                nc.vector.tensor_tensor(out=rows, in0=rows, in1=a_t[n][:, m0:m1], op=ALU.mult)
-            else:
-                nc.gpsimd.tensor_tensor(out=rows, in0=rows, in1=a_t[n][:, m0:m1], op=ALU.mult)
+            t_t[n] = mark_t[b][:, i, :]
+            engine = nc.vector if eng == "v" else nc.gpsimd
+            engine.tensor_tensor(out=t_t[n][:, m0:m1], in0=mark_t[b][:, i, m0:m1], in1=a_t[n][:, m0:m1], op=ALU.mult)
 
         def make_z(n, m0, m1):
             b, i = divmod(n, 4)
-            rows = mark_t[b][:, i, m0:m1]
             nc.vector.scalar_tensor_tensor(
-                out=rows, in0=hp_t[n][:, m0:m1], scalar=gain_t[:, b, i : i + 1], in1=rows, op0=ALU.mult, op1=ALU.add
+                out=mark_t[b][:, i, m0:m1],
+                in0=hp_t[n][:, m0:m1],
+                scalar=gain_col[n],
+                in1=t_t[n][:, m0:m1],
+                op0=ALU.mult,
+                op1=ALU.add,
             )
 
         def weave(dst_tile, src, eng):
@@ -219,13 +254,13 @@ def tile_list_ringing_evenness_kernel(
             cols = slice(HALF * c, HALF * (c + 1))
             y = y_all[:, c]
             for t in range(4):
-                if t % 2 == 0:
+                if ["ssss","vsvs"][c][t] == "v":
                     nc.vector.tensor_copy(out=y[:, t, :], in_=y_bank[t, c][:])
                 else:
                     nc.scalar.copy(out=y[:, t, :], in_=y_bank[t, c][:])
             nc.sync.dma_start(out=out_0.rearrange("(p t) m -> p t m", t=4)[:, :, cols], in_=y)
             y_cast = casts.tile([P, 4 * HALF], BF16, name="cast", tag="cast", align_bytes=64)
-            weave(y_cast, y, "v")
+            weave(y_cast, y, "vv"[c])
             nc.vector.quantize_mx(out=y_codes[:, cols].bitcast(E4M3), scales=y_scales[:, cols], in_=y_cast[:])
             nc.sync.dma_start(
                 out=out_1[0].rearrange("p m t -> p (m t)").bitcast(I32)[:, cols], in_=y_codes[:, cols].bitcast(I32)
@@ -246,7 +281,6 @@ def tile_list_ringing_evenness_kernel(
         load_w1(0, 2)
         load_hall(0)
         nc.sync.dma_start(out=offs2_t[:], in_=offs2)
-        nc.sync.dma_start(out=gain_t[:], in_=gain.rearrange("(b p i) -> p b i", b=2, i=4))
         load_w4_words()
         load_hall(1)
         load_w1(1, 0)
@@ -256,75 +290,81 @@ def tile_list_ringing_evenness_kernel(
             if a == 0:
                 for c in range(2):
                     gather_scales(c)
-            cast_w1(0, a, 0, "v" if a == 2 else "s")
-            cast_w1(0, a, 1, "s")
+            cast_w1(0, a, 0, "v" if a == 2 else "s", False)
+            cast_w1(0, a, 1, "s", False)
             for u in range(2):
-                quant_w1(0, a, u)
-                for i in range(2):
-                    for c in range(2):
-                        mm1(2 * u + i, a, c)
+                quant_w1(0, a, u, "c0%d%d" % (a, u))
+        for n in range(4):
+            for a in range(3):
+                for c in range(2):
+                    mm1(n, a, c)
         deal_w4_words()
-        load_mark(0)
+
+
         load_hall(2)
-        load_mark(1)
         load_w1(1, 1)
         load_hall(3)
-        load_mark(2)
         load_w1(1, 2)
-        load_mark(3)
         load_hall(4)
         load_hall(5)
-        load_mark(4)
-        load_hall(6)
-        load_mark(5)
-        load_hall(7)
-        load_mark(6)
-        load_mark(7)
         load_w4_scales()
-        cast_engine = "vsvsvs"
+        for a in range(2):
+            for u in range(2):
+                cast_w1(1, a, u, "g", True)
         for n in range(8):
+            if n == 4:
+                cast_w1(1, 2, 0, "v", False)
+                cast_w1(1, 2, 1, "s", False)
+                load_marks(0)
+                load_hall(6)
+                load_hall(7)
+                load_marks(1)
+                quant_w1(1, 0, None, "hall2")
+                quant_w1(1, 1, None, "hall3")
+                quant_w1(1, 2, 0, "c120")
+                quant_w1(1, 2, 1, "c121")
+                for k in range(4):
+                    marked(k, 0, M, "g")
             if n >= 4:
                 for a in range(3):
                     for c in range(2):
                         mm1(n, a, c)
             make_h(n)
+            make_top(n)
             alloc_looks(n)
             if n < 7:
                 look_copy(n, 0, M)
                 look_exp(n, 0, M)
-                marked(n, 0, M, "g")
             else:
                 for c in range(2):
                     look_copy(n, HALF * c, HALF * (c + 1))
                 for c in range(2):
                     look_exp(n, HALF * c, HALF * (c + 1))
-            if 1 <= n <= 3:
-                for u in range(2):
-                    cast_w1(1, n - 1, u, cast_engine[2 * (n - 1) + u])
-            if n >= 3:
-                make_z(n - 3, 0, M)
-            if 1 <= n <= 3:
-                quant_w1(1, n - 1, 0)
-            if 2 <= n <= 4:
-                quant_w1(1, n - 2, 1)
-            if n == 6:
-                for c in range(2):
-                    cast_z(0, c, "s")
-            if n == 7:
-                deal_w4_scales()
-                for c in range(2):
-                    quant_z(0, c)
+            if 4 <= n <= 6:
+                marked(n, 0, M, "g")
+            if n == 5:
+                load_gain_late()
+        for k in range(4):
+            make_z(k, 0, M)
         for c in range(2):
-            for t in range(4):
-                mm2(0, t, c)
-        for n in range(8 - 3, 7):
-            make_z(n, 0, M)
+            cast_z(0, c, "ss"[c])
+        deal_w4_scales()
+        for k in range(7, 7):
+            marked(k, 0, M, "v")
+        for k in range(4, 7):
+            make_z(k, 0, M)
         for c in range(2):
             marked(7, HALF * c, HALF * (c + 1), "v")
+        for c in range(2):
             make_z(7, HALF * c, HALF * (c + 1))
-            cast_z(1, c, "v" if c == 0 else "s")
+        for c in range(2):
+            cast_z(1, c, "vs"[c])
+        for c in range(2):
+            quant_z(0, c)
+            for t in range(4):
+                mm2(0, t, c)
             quant_z(1, c)
-        y_all = raws.tile([P, 2, 4, HALF], F32, name="raw", tag="raw")
+        y_all = keep.tile([P, 2, 4, HALF], F32, name="raw", tag="raw0", align_bytes=64)
         for c in range(2):
             for t in range(4):
                 mm2(1, t, c)

@@ -15,11 +15,16 @@ E4M3 = mybir.dt.float8_e4m3fn_x4
 E2M1 = mybir.dt.float4_e2m1fn_x4
 ALU = mybir.AluOpType
 ACT = mybir.ActivationFunctionType
-AX = mybir.AxisListType
 
 P = 128
+PASS = 512
 BANK = 512
 HALF = 256
+PAIR = 2 * P
+K_PASSES = K // PASS
+ROW_TILES = H // P
+W1_SLOTS = 4
+ROUND_BUFS = 6
 
 
 def tile_list_ringing_evenness_kernel(
@@ -28,347 +33,343 @@ def tile_list_ringing_evenness_kernel(
     nc = tc.nc
     with ExitStack() as ctx:
         keep = ctx.enter_context(tc.tile_pool(name="keep", bufs=1))
-        casts = ctx.enter_context(tc.tile_pool(name="casts", bufs=6))
-        hs = ctx.enter_context(tc.tile_pool(name="hs", bufs=6))
+        rounded = ctx.enter_context(tc.tile_pool(name="rounded", bufs=ROUND_BUFS))
         psum = ctx.enter_context(tc.psum_pool(name="psum", bufs=1))
 
         offs_t = keep.tile([P, S // 16], U16, name="offs_t")
         offs2_t = keep.tile([P, M // 16], U16, name="offs2_t")
-        tab_t = [keep.tile([P, T], U32, name="tab%d" % a) for a in range(3)]
+        tab_t = [keep.tile([P, T], U32, name="tab%d" % a) for a in range(K_PASSES)]
         tab_s = keep.tile([P, T], U8, name="tab_s")
-        v_words = [[keep.tile([P, BANK], U32, name="vw%d%d" % (a, c), align_bytes=64) for c in range(2)] for a in range(3)]
-        v_scales = [keep.tile([P, BANK], U8, name="vs%d" % c, align_bytes=64) for c in range(2)]
-        w1_codes = {}
-        w1_scales = {}
-        hall_t = [keep.tile([P, S], F32, name="hall%d" % n, tag="hall%d" % n, align_bytes=64) for n in range(8)]
-        gain_col = {}
-        ntop = [keep.tile([P, 1], F32, name="ntop%d" % n) for n in range(8)]
-        top = [keep.tile([P, 1], F32, name="top%d" % n) for n in range(8)]
+        v_words = [
+            [keep.tile([P, BANK], U32, name="v_words%d%d" % (a, c), align_bytes=64) for c in range(2)]
+            for a in range(K_PASSES)
+        ]
+        v_scales = [keep.tile([P, BANK], U8, name="v_scales%d" % c, align_bytes=64) for c in range(2)]
+        wide = keep.tile([P, 16 * PAIR], BF16, name="wide", tag="wide", align_bytes=64)
+        hall_t = [keep.tile([P, S], F32, name="hall%d" % n, tag="hall%d" % n, align_bytes=64) for n in range(ROW_TILES)]
+        minus_top = [keep.tile([P, 1], F32, name="minus_top%d" % n) for n in range(ROW_TILES)]
+        minus_h = keep.tile([P, S], F32, name="minus_h")
         w4_raw = keep.tile([P, 2, N], U16, name="w4_raw")
         w4s_raw = keep.tile([P, 2 * N], U8, name="w4s_raw")
-        w4_t = keep.tile([P, 2 * N], U16, name="w4_t", align_bytes=64)
-        w4s_t = keep.tile([P, 2 * N], U8, name="w4s_t", align_bytes=64)
-        z_codes = [[keep.tile([P, HALF], U32, name="zc%d%d" % (b, c), align_bytes=64) for c in range(2)] for b in range(2)]
-        z_scales = [[keep.tile([P, HALF], U8, name="zs%d%d" % (b, c), align_bytes=64) for c in range(2)] for b in range(2)]
+        w4_dealt = keep.tile([P, 2 * N], U16, name="w4_dealt", align_bytes=64)
+        z_codes = [[keep.tile([P, HALF], U32, name="z_codes%d%d" % (b, c), align_bytes=64) for c in range(2)] for b in range(2)]
+        z_scales = [[keep.tile([P, HALF], U8, name="z_scales%d%d" % (b, c), align_bytes=64) for c in range(2)] for b in range(2)]
         y_codes = keep.tile([P, M], U32, name="y_codes", align_bytes=64)
         y_scales = keep.tile([P, M], U8, name="y_scales", align_bytes=64)
 
-        w1_raw = {}
-        w1_cast = {}
-        mark_t = {}
-        h_t = {}
-        a_t = {}
-        hp_t = {}
-        h_bank = {}
-        y_bank = {}
-        z_cast = {}
-        t_t = {}
+        w1_raw, w1_bf16, w1_codes, w1_scales = {}, {}, {}, {}
+        mark_z = {}
+        gain_col, h_bank, h_t, look, plain, marked, z_bf16, y_bank = {}, {}, {}, {}, {}, {}, {}, {}
 
         def load_tab(a):
             nc.sync.dma_start(out=tab_t[a][:].bitcast(I32), in_=tab_words[a].rearrange("p t i -> p (t i)").bitcast(I32))
 
         def load_w1(b, a):
-            w1_raw[b, a] = keep.tile([P, 4, BANK], F32, name="raw", tag="raw%d" % ((3 * b + a) % 4), align_bytes=64)
+            slot = "w1_slot%d" % ((K_PASSES * b + a) % W1_SLOTS)
+            w1_raw[b, a] = keep.tile([P, 4, PASS], F32, name="w1_raw", tag=slot, align_bytes=64)
             nc.sync.dma_start(
                 out=w1_raw[b, a][:],
-                in_=w1[512 * a : 512 * (a + 1), 512 * b : 512 * (b + 1)].rearrange("(p j) c -> p j c", j=4),
+                in_=w1[PASS * a : PASS * (a + 1), PASS * b : PASS * (b + 1)].rearrange("(p j) c -> p j c", j=4),
             )
 
         def load_hall(n):
             b, i = divmod(n, 4)
             nc.sync.dma_start(
-                out=hall_t[n][:], in_=hall[512 * b : 512 * (b + 1), :].rearrange("(p i) s -> p i s", i=4)[:, i, :]
+                out=hall_t[n][:], in_=hall[PASS * b : PASS * (b + 1), :].rearrange("(p i) s -> p i s", i=4)[:, i, :]
             )
 
-        def load_marks(b):
-            mark_t[b] = keep.tile([P, 4, M], F32, name="raw", tag=["raw2","raw3"][b], align_bytes=64)
-            nc.sync.dma_start(out=mark_t[b][:], in_=mark[512 * b : 512 * (b + 1), :].rearrange("(p i) m -> p i m", i=4))
+        def load_mark(b, first, count):
+            if first == 0:
+                mark_z[b] = keep.tile([P, 4, M], F32, name="mark_z", tag="w1_slot%d" % (2 + b), align_bytes=64)
+            rows = mark[PASS * b : PASS * (b + 1), :].rearrange("(p i) m -> p i m", i=4)
+            nc.sync.dma_start(out=mark_z[b][:, first : first + count, :], in_=rows[:, first : first + count, :])
 
-        def load_mark(n):
-            b, i = divmod(n, 4)
-            if i == 0:
-                mark_t[b] = keep.tile([P, 4, M], F32, name="raw", tag=["raw2","raw3"][b], align_bytes=64)
+        def load_gain(first, count, slot):
+            cols = keep.tile([P, count], F32, name="gain", tag=slot, align_bytes=64)
+            b, i = divmod(first, 4)
             nc.sync.dma_start(
-                out=mark_t[b][:, i, :], in_=mark[512 * b : 512 * (b + 1), :].rearrange("(p i) m -> p i m", i=4)[:, i, :]
+                out=cols[:], in_=gain[PASS * b : PASS * (b + 1)].rearrange("(p i) -> p i", i=4)[:, i : i + count]
             )
+            for k in range(count):
+                gain_col[first + k] = cols[:, k : k + 1]
 
-        def load_w4_words():
-            nc.sync.dma_start(out=w4_raw[:].bitcast(I32), in_=w4_words.bitcast(I32).rearrange("a p c -> p a c"))
-
-        def load_w4_scales():
-            for q in range(4):
-                nc.sync.dma_start(
-                    out=w4s_raw[32 * q : 32 * q + 4, :].bitcast(I32).rearrange("r (a c) -> r a c", a=2),
-                    in_=w4_scales[:, 4 * q : 4 * q + 4, :].bitcast(I32).rearrange("a r c -> r a c"),
-                )
-
-        def deal_w4_words():
-            nc.scalar.copy(
-                out=w4_t[:].rearrange("p (a t q) -> p a t q", a=2, t=4),
-                in_=w4_raw[:].rearrange("p a (q t) -> p a t q", t=4),
-            )
-
-        def deal_w4_scales():
-            nc.vector.tensor_copy(
-                out=w4s_t[:].rearrange("p (a t q) -> p a t q", a=2, t=4),
-                in_=w4s_raw[:].rearrange("p (a q t) -> p a t q", a=2, t=4),
-            )
-
-        def gather_words(a, c):
-            nc.vector.tensor_copy(out=v_words[a][c][:], in_=tab_t[a][:].indirect(offs_t[:, 32 * c : 32 * (c + 1)]))
-
-        def gather_scales(c):
-            nc.vector.tensor_copy(out=v_scales[c][:], in_=tab_s[:].indirect(offs_t[:, 32 * c : 32 * (c + 1)]))
-
-        def cast_w1(b, a, u, eng, joint):
-            if not joint:
-                w1_cast[b, a, u] = casts.tile([P, 1024], BF16, name="cast", tag="cast", align_bytes=64)[:]
-            elif u == 0:
-                both = casts.tile([P, 2048], BF16, name="cast2", tag="cast2", bufs=2, align_bytes=64)
-                w1_cast[b, a] = both[:]
-                w1_cast[b, a, 0] = both[:, 0:1024]
-                w1_cast[b, a, 1] = both[:, 1024:2048]
-            dst = w1_cast[b, a, u].rearrange("p (t m j) -> p m j t", t=2, j=4)
-            src = w1_raw[b, a][:].rearrange("p j (m t) -> p m j t", t=4)[:, :, :, 2 * u : 2 * u + 2]
-            if eng == "v":
-                nc.vector.tensor_copy(out=dst, in_=src)
-            elif eng == "s":
-                nc.scalar.activation(out=dst, in_=src, func=ACT.Copy)
-            else:
+        def round_w1(b, a, u, engine, slot=None):
+            if engine == "gpsimd":
+                w1_bf16[b, a, u] = wide[:, 4 * PAIR * (2 * a + u) : 4 * PAIR * (2 * a + u + 1)]
                 nc.gpsimd.tensor_scalar(
-                    out=w1_cast[b, a, u].rearrange("p (t m j) -> p m t j", t=2, j=4),
+                    out=w1_bf16[b, a, u].rearrange("p (t m j) -> p m t j", t=2, j=4),
                     in0=w1_raw[b, a][:].rearrange("p j (m t) -> p m t j", t=4)[:, :, 2 * u : 2 * u + 2, :],
                     scalar1=1.0,
                     scalar2=0.0,
                     op0=ALU.mult,
                     op1=ALU.add,
                 )
-
-        def quant_w1(b, a, u, tag):
-            width = BANK if u is None else HALF
-            codes = keep.tile([P, width], U32, name="codes", tag=tag, align_bytes=64)
-            scales = keep.tile([P, width], U8, name="scales", tag="s" + tag, align_bytes=64)
-            if u is None:
-                for k in range(2):
-                    w1_codes[b, a, k] = codes[:, HALF * k : HALF * (k + 1)]
-                    w1_scales[b, a, k] = scales[:, HALF * k : HALF * (k + 1)]
-                rounded = w1_cast[b, a]
+                return
+            if slot is None:
+                unit = rounded.tile([P, 4 * PAIR], BF16, name="rounded", tag="rounded", align_bytes=64)
             else:
-                w1_codes[b, a, u] = codes[:]
-                w1_scales[b, a, u] = scales[:]
-                rounded = w1_cast[b, a, u]
-            nc.vector.quantize_mx(out=codes[:].bitcast(E4M3), scales=scales[:], in_=rounded)
+                unit = keep.tile([P, 4 * PAIR], BF16, name="rounded", tag=slot, align_bytes=64)
+            w1_bf16[b, a, u] = unit[:]
+            dst = unit[:].rearrange("p (t m j) -> p m j t", t=2, j=4)
+            src = w1_raw[b, a][:].rearrange("p j (m t) -> p m j t", t=4)[:, :, :, 2 * u : 2 * u + 2]
+            round_copy(engine, dst, src)
 
-        def mm1(n, a, c):
-            b, i = divmod(n, 4)
-            if a == 0:
-                h_bank[n, c] = psum.tile([P, BANK], F32, name="bank", tag="bank%d" % (2 * i + c))
-            cols = slice(P * (i % 2), P * (i % 2 + 1))
-            nc.tensor.matmul_mx(
-                out=h_bank[n, c][:],
-                lhsT=w1_codes[b, a, i // 2][:, cols].bitcast(E4M3),
-                lhsT_scale=w1_scales[b, a, i // 2][:, cols],
-                rhs=v_words[a][c][:].bitcast(E4M3),
-                rhs_scale=v_scales[c][4 * a : P, :],
-                start=(a == 0),
-                stop=(a == 2),
-            )
-
-        def load_gain_late():
-            late = keep.tile([P, 2, 4], F32, name="gain_late", tag="hall5", align_bytes=64)
-            nc.sync.dma_start(out=late[:], in_=gain.rearrange("(b p i) -> p b i", b=2, i=4))
-            for n in range(8):
-                gain_col[n] = late[:, n // 4, n % 4 : n % 4 + 1]
-
-        def make_h(n):
-            for c in range(2):
-                cols = slice(BANK * c, BANK * (c + 1))
-                nc.vector.tensor_tensor(out=hall_t[n][:, cols], in0=h_bank[n, c][:], in1=hall_t[n][:, cols], op=ALU.mult)
-
-        def make_top(n):
-            h_t[n] = hs.tile([P, S], F32, name="h", tag="h")
-            nc.vector.tensor_scalar(
-                out=h_t[n][:], in0=hall_t[n][:], scalar1=1.0, scalar2=None, op0=ALU.mult, op1=ALU.max, accum_out=top[n][:]
-            )
-            nc.scalar.activation(out=ntop[n][:], in_=top[n][:], func=ACT.Copy, scale=-1.0)
-
-        def alloc_looks(n):
-            a_t[n] = keep.tile([P, M], F32, name="a", tag="a%d" % n, align_bytes=64)[:]
-            hp_t[n] = keep.tile([P, M], F32, name="hp", tag="hp%d" % n, align_bytes=64)[:]
-
-        def look_copy(n, m0, m1):
-            nc.scalar.activation(out=hp_t[n][:, m0:m1], in_=h_t[n][:].indirect(offs2_t[:, m0 // 16 : m1 // 16]), func=ACT.Copy)
-
-        def look_exp(n, m0, m1):
-            nc.scalar.activation(
-                out=a_t[n][:, m0:m1], in_=h_t[n][:].indirect(offs2_t[:, m0 // 16 : m1 // 16]), func=ACT.Exp, bias=ntop[n][:]
-            )
-
-        def marked(n, m0, m1, eng):
-            b, i = divmod(n, 4)
-            t_t[n] = mark_t[b][:, i, :]
-            engine = nc.vector if eng == "v" else nc.gpsimd
-            engine.tensor_tensor(out=t_t[n][:, m0:m1], in0=mark_t[b][:, i, m0:m1], in1=a_t[n][:, m0:m1], op=ALU.mult)
-
-        def make_z(n, m0, m1):
-            b, i = divmod(n, 4)
-            nc.vector.scalar_tensor_tensor(
-                out=mark_t[b][:, i, m0:m1],
-                in0=hp_t[n][:, m0:m1],
-                scalar=gain_col[n],
-                in1=t_t[n][:, m0:m1],
-                op0=ALU.mult,
-                op1=ALU.add,
-            )
-
-        def weave(dst_tile, src, eng):
-            dst = dst_tile[:].rearrange("p (c i t) -> p c t i", i=4, t=4)
-            src = src.rearrange("p t (c i) -> p c t i", i=4)
-            if eng == "v":
+        def round_copy(engine, dst, src):
+            if engine == "vector":
                 nc.vector.tensor_copy(out=dst, in_=src)
             else:
                 nc.scalar.activation(out=dst, in_=src, func=ACT.Copy)
 
-        def cast_z(b, c, eng):
-            z_cast[b, c] = casts.tile([P, 4 * HALF], BF16, name="cast", tag="cast", align_bytes=64)
-            weave(z_cast[b, c], mark_t[b][:, :, HALF * c : HALF * (c + 1)], eng)
+        def quantise_w1(b, a, u, slot):
+            codes = keep.tile([P, PAIR], U32, name="w1_codes", tag=slot, align_bytes=64)
+            scales = keep.tile([P, PAIR], U8, name="w1_scales", tag="scales_" + slot, align_bytes=64)
+            w1_codes[b, a, u] = codes[:]
+            w1_scales[b, a, u] = scales[:]
+            nc.vector.quantize_mx(out=codes[:].bitcast(E4M3), scales=scales[:], in_=w1_bf16[b, a, u])
 
-        def quant_z(b, c):
-            nc.vector.quantize_mx(out=z_codes[b][c][:].bitcast(E4M3), scales=z_scales[b][c][:], in_=z_cast[b, c][:])
+        def quantise_wide():
+            codes = keep.tile([P, 4 * PAIR], U32, name="w1_codes", tag="hall3", align_bytes=64)
+            scales = keep.tile([P, 4 * PAIR], U8, name="wide_scales", align_bytes=64)
+            for k in range(4):
+                w1_codes[1, k // 2, k % 2] = codes[:, PAIR * k : PAIR * (k + 1)]
+                w1_scales[1, k // 2, k % 2] = scales[:, PAIR * k : PAIR * (k + 1)]
+            nc.vector.quantize_mx(out=codes[:].bitcast(E4M3), scales=scales[:], in_=wide[:])
 
-        def mm2(b, t, c):
-            if b == 0:
-                y_bank[t, c] = psum.tile([P, HALF], F32, name="bank", tag="bank%d" % (2 * t + c))
-            cols = slice(N * b + P * t, N * b + P * (t + 1))
-            nc.tensor.matmul_mx(
-                out=y_bank[t, c][:],
-                lhsT=w4_t[:, cols].bitcast(E2M1),
-                lhsT_scale=w4s_t[:, cols],
-                rhs=z_codes[b][c][:].bitcast(E4M3),
-                rhs_scale=z_scales[b][c][:],
-                start=(b == 0),
-                stop=(b == 1),
+        def first_product(n):
+            b, i = divmod(n, 4)
+            cols = slice(P * (i % 2), P * (i % 2 + 1))
+            for a in range(K_PASSES):
+                for c in range(2):
+                    if a == 0:
+                        h_bank[n, c] = psum.tile([P, BANK], F32, name="bank", tag="bank%d" % (2 * i + c))
+                    nc.tensor.matmul_mx(
+                        out=h_bank[n, c][:],
+                        lhsT=w1_codes[b, a, i // 2][:, cols].bitcast(E4M3),
+                        lhsT_scale=w1_scales[b, a, i // 2][:, cols],
+                        rhs=v_words[a][c][:].bitcast(E4M3),
+                        rhs_scale=v_scales[c][4 * a : P, :],
+                        start=(a == 0),
+                        stop=(a == K_PASSES - 1),
+                    )
+
+        def make_h(n):
+            h_t[n] = keep.tile([P, S], F32, name="h", tag="h%d" % n, align_bytes=64)
+            for c in range(2):
+                cols = slice(BANK * c, BANK * (c + 1))
+                nc.vector.tensor_tensor(out=h_t[n][:, cols], in0=h_bank[n, c][:], in1=hall_t[n][:, cols], op=ALU.mult)
+
+        def make_top(n):
+            nc.vector.tensor_scalar(
+                out=minus_h[:],
+                in0=h_t[n][:],
+                scalar1=-1.0,
+                scalar2=None,
+                op0=ALU.mult,
+                op1=ALU.min,
+                accum_out=minus_top[n][:],
             )
 
-        def finish(c, y_all):
-            cols = slice(HALF * c, HALF * (c + 1))
-            y = y_all[:, c]
+        def looks(n, parts):
+            look[n] = keep.tile([P, M], F32, name="look", tag="look%d" % n, align_bytes=64)
+            plain[n] = keep.tile([P, M], F32, name="plain", tag="plain%d" % n, align_bytes=64)
+            width = M // parts
+            for m in range(0, M, width):
+                window = h_t[n][:].indirect(offs2_t[:, m // 16 : (m + width) // 16])
+                nc.scalar.activation(out=plain[n][:, m : m + width], in_=window, func=ACT.Copy)
+            for m in range(0, M, width):
+                window = h_t[n][:].indirect(offs2_t[:, m // 16 : (m + width) // 16])
+                nc.scalar.activation(out=look[n][:, m : m + width], in_=window, func=ACT.Exp, bias=minus_top[n][:])
+
+        def place_marked(first, count, slot):
+            held = keep.tile([P, count, M], F32, name="marked", tag=slot, align_bytes=64)
+            for k in range(count):
+                marked[first + k] = held[:, k, :]
+
+        def mark_look(n, engine, cols=slice(0, M)):
+            b, i = divmod(n, 4)
+            engine.tensor_tensor(out=marked[n][:, cols], in0=mark_z[b][:, i, cols], in1=look[n][:, cols], op=ALU.mult)
+
+        def make_z(n, cols=slice(0, M)):
+            b, i = divmod(n, 4)
+            nc.vector.scalar_tensor_tensor(
+                out=mark_z[b][:, i, cols],
+                in0=plain[n][:, cols],
+                scalar=gain_col[n],
+                in1=marked[n][:, cols],
+                op0=ALU.mult,
+                op1=ALU.add,
+            )
+
+        def interleave(engine, rows):
+            unit = rounded.tile([P, 4 * HALF], BF16, name="rounded", tag="rounded", align_bytes=64)
+            dst = unit[:].rearrange("p (c i t) -> p c t i", i=4, t=4)
+            round_copy(engine, dst, rows.rearrange("p t (c i) -> p c t i", i=4))
+            return unit
+
+        def half(c):
+            return slice(HALF * c, HALF * (c + 1))
+
+        def quantise_z(b, c):
+            nc.vector.quantize_mx(out=z_codes[b][c][:].bitcast(E4M3), scales=z_scales[b][c][:], in_=z_bf16[b, c][:])
+
+        def second_product(b, c):
             for t in range(4):
-                if ["ssss","vsvs"][c][t] == "v":
+                if b == 0:
+                    y_bank[t, c] = psum.tile([P, HALF], F32, name="bank", tag="bank%d" % (2 * t + c))
+                cols = slice(N * b + P * t, N * b + P * (t + 1))
+                nc.tensor.matmul_mx(
+                    out=y_bank[t, c][:],
+                    lhsT=w4_dealt[:, cols].bitcast(E2M1),
+                    lhsT_scale=w4s_dealt[:, cols],
+                    rhs=z_codes[b][c][:].bitcast(E4M3),
+                    rhs_scale=z_scales[b][c][:],
+                    start=(b == 0),
+                    stop=(b == 1),
+                )
+
+        def hand_out(c, y):
+            for t in range(4):
+                if t % 2 == 0:
                     nc.vector.tensor_copy(out=y[:, t, :], in_=y_bank[t, c][:])
                 else:
                     nc.scalar.copy(out=y[:, t, :], in_=y_bank[t, c][:])
-            nc.sync.dma_start(out=out_0.rearrange("(p t) m -> p t m", t=4)[:, :, cols], in_=y)
-            y_cast = casts.tile([P, 4 * HALF], BF16, name="cast", tag="cast", align_bytes=64)
-            weave(y_cast, y, "vv"[c])
-            nc.vector.quantize_mx(out=y_codes[:, cols].bitcast(E4M3), scales=y_scales[:, cols], in_=y_cast[:])
+            nc.sync.dma_start(out=out_0.rearrange("(p t) m -> p t m", t=4)[:, :, half(c)], in_=y)
+            y_bf16 = interleave("vector", y)
+            nc.vector.quantize_mx(out=y_codes[:, half(c)].bitcast(E4M3), scales=y_scales[:, half(c)], in_=y_bf16[:])
             nc.sync.dma_start(
-                out=out_1[0].rearrange("p m t -> p (m t)").bitcast(I32)[:, cols], in_=y_codes[:, cols].bitcast(I32)
+                out=out_1[0].rearrange("p m t -> p (m t)").bitcast(I32)[:, half(c)], in_=y_codes[:, half(c)].bitcast(I32)
             )
 
         nc.gpsimd.memset(tab_s[:].bitcast(I32), 0)
         nc.gpsimd.memset(w4s_raw[:].bitcast(I32), 0)
+        for q in range(4):
+            nc.gpsimd.dma_start(
+                out=w4s_raw[32 * q : 32 * q + 4, :].bitcast(I32).rearrange("r (b c) -> r b c", b=2),
+                in_=w4_scales[:, 4 * q : 4 * q + 4, :].bitcast(I32).rearrange("b r c -> r b c"),
+            )
         load_tab(0)
         nc.sync.dma_start(out=offs_t[:], in_=offs)
         load_w1(0, 0)
         for q in range(4):
             nc.sync.dma_start(
-                out=tab_s[32 * q : 32 * q + 12, :].bitcast(I32), in_=tab_scales[:, 4 * q : 4 * q + 4, :].bitcast(I32)
+                out=tab_s[32 * q : 32 * q + 4 * K_PASSES, :].bitcast(I32),
+                in_=tab_scales[:, 4 * q : 4 * q + 4, :].bitcast(I32),
             )
-        load_tab(1)
-        load_w1(0, 1)
-        load_tab(2)
-        load_w1(0, 2)
+        for a in range(1, K_PASSES):
+            load_tab(a)
+            load_w1(0, a)
         load_hall(0)
         nc.sync.dma_start(out=offs2_t[:], in_=offs2)
-        load_w4_words()
+        nc.sync.dma_start(out=w4_raw[:].bitcast(I32), in_=w4_words.bitcast(I32).rearrange("b p c -> p b c"))
         load_hall(1)
         load_w1(1, 0)
-        for a in range(3):
+
+        for a in range(K_PASSES):
+            last = a == K_PASSES - 1
             for c in range(2):
-                gather_words(a, c)
+                nc.vector.tensor_copy(out=v_words[a][c][:], in_=tab_t[a][:].indirect(offs_t[:, 32 * c : 32 * (c + 1)]))
             if a == 0:
                 for c in range(2):
-                    gather_scales(c)
-            cast_w1(0, a, 0, "v" if a == 2 else "s", False)
-            cast_w1(0, a, 1, "s", False)
+                    nc.vector.tensor_copy(out=v_scales[c][:], in_=tab_s[:].indirect(offs_t[:, 32 * c : 32 * (c + 1)]))
+            round_w1(0, a, 0, "vector" if last else "scalar")
+            round_w1(0, a, 1, "scalar", "head_unit" if last else None)
             for u in range(2):
-                quant_w1(0, a, u, "c0%d%d" % (a, u))
+                quantise_w1(0, a, u, "w1_codes%d%d" % (a, u))
         for n in range(4):
-            for a in range(3):
-                for c in range(2):
-                    mm1(n, a, c)
-        deal_w4_words()
+            first_product(n)
 
-
-        load_hall(2)
-        load_w1(1, 1)
-        load_hall(3)
-        load_w1(1, 2)
-        load_hall(4)
-        load_hall(5)
-        load_w4_scales()
+        nc.scalar.copy(
+            out=w4_dealt[:].rearrange("p (b t q) -> p b t q", b=2, t=4),
+            in_=w4_raw[:].rearrange("p b (q t) -> p b t q", t=4),
+        )
+        for a in range(1, K_PASSES):
+            load_hall(1 + a)
+            load_w1(1, a)
+        load_gain(0, 2, "gain0")
+        load_gain(4, 4, "gain4")
+        w4s_dealt = keep.tile([P, 2 * N], U8, name="w4s_dealt", tag="head_unit", align_bytes=64)
+        nc.gpsimd.tensor_copy(
+            out=w4s_dealt[:].rearrange("p (b t q) -> p b t q", b=2, t=4),
+            in_=w4s_raw[:].rearrange("p (b q t) -> p b t q", b=2, t=4),
+        )
         for a in range(2):
             for u in range(2):
-                cast_w1(1, a, u, "g", True)
-        for n in range(8):
-            if n == 4:
-                cast_w1(1, 2, 0, "v", False)
-                cast_w1(1, 2, 1, "s", False)
-                load_marks(0)
-                load_hall(6)
-                load_hall(7)
-                load_marks(1)
-                quant_w1(1, 0, None, "hall2")
-                quant_w1(1, 1, None, "hall3")
-                quant_w1(1, 2, 0, "c120")
-                quant_w1(1, 2, 1, "c121")
-                for k in range(4):
-                    marked(k, 0, M, "g")
-            if n >= 4:
-                for a in range(3):
-                    for c in range(2):
-                        mm1(n, a, c)
+                round_w1(1, a, u, "gpsimd")
+
+        for n in range(4):
             make_h(n)
             make_top(n)
-            alloc_looks(n)
-            if n < 7:
-                look_copy(n, 0, M)
-                look_exp(n, 0, M)
-            else:
-                for c in range(2):
-                    look_copy(n, HALF * c, HALF * (c + 1))
-                for c in range(2):
-                    look_exp(n, HALF * c, HALF * (c + 1))
-            if 4 <= n <= 6:
-                marked(n, 0, M, "g")
-            if n == 5:
-                load_gain_late()
-        for k in range(4):
-            make_z(k, 0, M)
+            looks(n, 1)
+
+        quantise_wide()
+        round_w1(1, 2, 0, "scalar")
+        round_w1(1, 2, 1, "scalar", "last_unit")
+        load_mark(0, 0, 2)
+        load_hall(4)
+        load_mark(0, 2, 2)
+        for n in range(5, ROW_TILES):
+            load_hall(n)
+        load_mark(1, 0, 4)
+        place_marked(0, 2, "wide")
+        for n in range(2):
+            mark_look(n, nc.vector)
+        quantise_w1(1, 2, 0, "look0")
+        for n in range(2):
+            make_z(n)
+        quantise_w1(1, 2, 1, "plain1")
+        place_marked(2, 2, "last_unit")
+        for n in range(2, 4):
+            mark_look(n, nc.gpsimd)
+
+        first_product(4)
+        make_h(4)
+        make_top(4)
+        looks(4, 1)
+        load_gain(2, 2, "hall4")
+
+        first_product(5)
+        make_h(5)
+        make_top(5)
+        looks(5, 1)
+        for n in range(2, 4):
+            make_z(n)
         for c in range(2):
-            cast_z(0, c, "ss"[c])
-        deal_w4_scales()
-        for k in range(7, 7):
-            marked(k, 0, M, "v")
-        for k in range(4, 7):
-            make_z(k, 0, M)
+            z_bf16[0, c] = interleave("scalar", mark_z[0][:, :, half(c)])
+        place_marked(4, 1, "plain3")
+        mark_look(4, nc.gpsimd)
+
+        first_product(6)
+        make_h(6)
+        place_marked(5, 1, "hall6")
+        mark_look(5, nc.vector)
+        make_top(6)
+        looks(6, 1)
+
+        first_product(7)
+        make_h(7)
+        make_top(7)
+        looks(7, 2)
+
         for c in range(2):
-            marked(7, HALF * c, HALF * (c + 1), "v")
+            quantise_z(0, c)
+            second_product(0, c)
+        for n in range(4, 6):
+            make_z(n)
+        for n in range(6, ROW_TILES):
+            marked[n] = mark_z[1][:, n - 4, :]
+        mark_look(6, nc.vector)
         for c in range(2):
-            make_z(7, HALF * c, HALF * (c + 1))
+            mark_look(7, nc.vector, half(c))
+        make_z(6)
         for c in range(2):
-            cast_z(1, c, "vs"[c])
+            make_z(7, half(c))
         for c in range(2):
-            quant_z(0, c)
-            for t in range(4):
-                mm2(0, t, c)
-            quant_z(1, c)
-        y_all = keep.tile([P, 2, 4, HALF], F32, name="raw", tag="raw0", align_bytes=64)
+            z_bf16[1, c] = interleave("vector" if c == 0 else "scalar", mark_z[1][:, :, half(c)])
+            quantise_z(1, c)
+        y_halves = keep.tile([P, 2, 4, HALF], F32, name="y_halves", tag="w1_slot0", align_bytes=64)
         for c in range(2):
-            for t in range(4):
-                mm2(1, t, c)
-            finish(c, y_all)
+            second_product(1, c)
+            hand_out(c, y_halves[:, c])
         for q in range(4):
             queue = nc.sync if q % 2 == 0 else nc.scalar
             queue.dma_start(

from contextlib import ExitStack

import concourse.mybir as mybir

K, T, S, M, H, N = 1536, 2048, 1024, 512, 1024, 512
FLOPS = 2 * K * H * S + 2 * H * N * M

F32 = mybir.dt.float32
BF16 = mybir.dt.bfloat16
I32 = mybir.dt.int32
U32 = mybir.dt.uint32
U16 = mybir.dt.uint16
U8 = mybir.dt.uint8
E4M3 = mybir.dt.float8_e4m3fn_x4
E2M1 = mybir.dt.float4_e2m1fn_x4
ALU = mybir.AluOpType
ACT = mybir.ActivationFunctionType

P = 128
PASS = 512
BANK = 512
HALF = 256
PAIR = 2 * P
K_PASSES = K // PASS
ROW_TILES = H // P
W1_SLOTS = 4
ROUND_BUFS = 6


def tile_list_ringing_evenness_kernel(
    tc, tab_words, tab_scales, offs, offs2, w1, hall, mark, gain, w4_words, w4_scales, out_0, out_1, out_2
):
    nc = tc.nc
    with ExitStack() as ctx:
        keep = ctx.enter_context(tc.tile_pool(name="keep", bufs=1))
        rounded = ctx.enter_context(tc.tile_pool(name="rounded", bufs=ROUND_BUFS))
        psum = ctx.enter_context(tc.psum_pool(name="psum", bufs=1))

        offs_t = keep.tile([P, S // 16], U16, name="offs_t")
        offs2_t = keep.tile([P, M // 16], U16, name="offs2_t")
        tab_t = [keep.tile([P, T], U32, name="tab%d" % a) for a in range(K_PASSES)]
        tab_s = keep.tile([P, T], U8, name="tab_s")
        v_words = [
            [keep.tile([P, BANK], U32, name="v_words%d%d" % (a, c), align_bytes=64) for c in range(2)]
            for a in range(K_PASSES)
        ]
        v_scales = [keep.tile([P, BANK], U8, name="v_scales%d" % c, align_bytes=64) for c in range(2)]
        wide = keep.tile([P, 16 * PAIR], BF16, name="wide", tag="wide", align_bytes=64)
        hall_t = [keep.tile([P, S], F32, name="hall%d" % n, tag="hall%d" % n, align_bytes=64) for n in range(ROW_TILES)]
        minus_top = [keep.tile([P, 1], F32, name="minus_top%d" % n) for n in range(ROW_TILES)]
        minus_h = keep.tile([P, S], F32, name="minus_h")
        w4_raw = keep.tile([P, 2, N], U16, name="w4_raw")
        w4s_raw = keep.tile([P, 2 * N], U8, name="w4s_raw")
        w4_dealt = keep.tile([P, 2 * N], U16, name="w4_dealt", align_bytes=64)
        z_codes = [[keep.tile([P, HALF], U32, name="z_codes%d%d" % (b, c), align_bytes=64) for c in range(2)] for b in range(2)]
        z_scales = [[keep.tile([P, HALF], U8, name="z_scales%d%d" % (b, c), align_bytes=64) for c in range(2)] for b in range(2)]
        y_codes = keep.tile([P, M], U32, name="y_codes", align_bytes=64)
        y_scales = keep.tile([P, M], U8, name="y_scales", align_bytes=64)

        w1_raw, w1_bf16, w1_codes, w1_scales = {}, {}, {}, {}
        mark_z = {}
        gain_col, h_bank, h_t, look, plain, marked, z_bf16, y_bank = {}, {}, {}, {}, {}, {}, {}, {}

        def load_tab(a):
            nc.sync.dma_start(out=tab_t[a][:].bitcast(I32), in_=tab_words[a].rearrange("p t i -> p (t i)").bitcast(I32))

        def load_w1(b, a):
            slot = "w1_slot%d" % ((K_PASSES * b + a) % W1_SLOTS)
            w1_raw[b, a] = keep.tile([P, 4, PASS], F32, name="w1_raw", tag=slot, align_bytes=64)
            nc.sync.dma_start(
                out=w1_raw[b, a][:],
                in_=w1[PASS * a : PASS * (a + 1), PASS * b : PASS * (b + 1)].rearrange("(p j) c -> p j c", j=4),
            )

        def load_hall(n):
            b, i = divmod(n, 4)
            nc.sync.dma_start(
                out=hall_t[n][:], in_=hall[PASS * b : PASS * (b + 1), :].rearrange("(p i) s -> p i s", i=4)[:, i, :]
            )

        def load_mark(b, first, count):
            if first == 0:
                mark_z[b] = keep.tile([P, 4, M], F32, name="mark_z", tag="w1_slot%d" % (2 + b), align_bytes=64)
            rows = mark[PASS * b : PASS * (b + 1), :].rearrange("(p i) m -> p i m", i=4)
            nc.sync.dma_start(out=mark_z[b][:, first : first + count, :], in_=rows[:, first : first + count, :])

        def load_gain(first, count, slot):
            cols = keep.tile([P, count], F32, name="gain", tag=slot, align_bytes=64)
            b, i = divmod(first, 4)
            nc.sync.dma_start(
                out=cols[:], in_=gain[PASS * b : PASS * (b + 1)].rearrange("(p i) -> p i", i=4)[:, i : i + count]
            )
            for k in range(count):
                gain_col[first + k] = cols[:, k : k + 1]

        def round_w1(b, a, u, engine, slot=None):
            if engine == "gpsimd":
                w1_bf16[b, a, u] = wide[:, 4 * PAIR * (2 * a + u) : 4 * PAIR * (2 * a + u + 1)]
                nc.gpsimd.tensor_scalar(
                    out=w1_bf16[b, a, u].rearrange("p (t m j) -> p m t j", t=2, j=4),
                    in0=w1_raw[b, a][:].rearrange("p j (m t) -> p m t j", t=4)[:, :, 2 * u : 2 * u + 2, :],
                    scalar1=1.0,
                    scalar2=0.0,
                    op0=ALU.mult,
                    op1=ALU.add,
                )
                return
            if slot is None:
                unit = rounded.tile([P, 4 * PAIR], BF16, name="rounded", tag="rounded", align_bytes=64)
            else:
                unit = keep.tile([P, 4 * PAIR], BF16, name="rounded", tag=slot, align_bytes=64)
            w1_bf16[b, a, u] = unit[:]
            dst = unit[:].rearrange("p (t m j) -> p m j t", t=2, j=4)
            src = w1_raw[b, a][:].rearrange("p j (m t) -> p m j t", t=4)[:, :, :, 2 * u : 2 * u + 2]
            round_copy(engine, dst, src)

        def round_copy(engine, dst, src):
            if engine == "vector":
                nc.vector.tensor_copy(out=dst, in_=src)
            else:
                nc.scalar.activation(out=dst, in_=src, func=ACT.Copy)

        def quantise_w1(b, a, u, slot):
            codes = keep.tile([P, PAIR], U32, name="w1_codes", tag=slot, align_bytes=64)
            scales = keep.tile([P, PAIR], U8, name="w1_scales", tag="scales_" + slot, align_bytes=64)
            w1_codes[b, a, u] = codes[:]
            w1_scales[b, a, u] = scales[:]
            nc.vector.quantize_mx(out=codes[:].bitcast(E4M3), scales=scales[:], in_=w1_bf16[b, a, u])

        def quantise_wide():
            codes = keep.tile([P, 4 * PAIR], U32, name="w1_codes", tag="hall3", align_bytes=64)
            scales = keep.tile([P, 4 * PAIR], U8, name="wide_scales", align_bytes=64)
            for k in range(4):
                w1_codes[1, k // 2, k % 2] = codes[:, PAIR * k : PAIR * (k + 1)]
                w1_scales[1, k // 2, k % 2] = scales[:, PAIR * k : PAIR * (k + 1)]
            nc.vector.quantize_mx(out=codes[:].bitcast(E4M3), scales=scales[:], in_=wide[:])

        def first_product(n):
            b, i = divmod(n, 4)
            cols = slice(P * (i % 2), P * (i % 2 + 1))
            for a in range(K_PASSES):
                for c in range(2):
                    if a == 0:
                        h_bank[n, c] = psum.tile([P, BANK], F32, name="bank", tag="bank%d" % (2 * i + c))
                    nc.tensor.matmul_mx(
                        out=h_bank[n, c][:],
                        lhsT=w1_codes[b, a, i // 2][:, cols].bitcast(E4M3),
                        lhsT_scale=w1_scales[b, a, i // 2][:, cols],
                        rhs=v_words[a][c][:].bitcast(E4M3),
                        rhs_scale=v_scales[c][4 * a : P, :],
                        start=(a == 0),
                        stop=(a == K_PASSES - 1),
                    )

        def make_h(n):
            h_t[n] = keep.tile([P, S], F32, name="h", tag="h%d" % n, align_bytes=64)
            for c in range(2):
                cols = slice(BANK * c, BANK * (c + 1))
                nc.vector.tensor_tensor(out=h_t[n][:, cols], in0=h_bank[n, c][:], in1=hall_t[n][:, cols], op=ALU.mult)

        def make_top(n):
            nc.vector.tensor_scalar(
                out=minus_h[:],
                in0=h_t[n][:],
                scalar1=-1.0,
                scalar2=None,
                op0=ALU.mult,
                op1=ALU.min,
                accum_out=minus_top[n][:],
            )

        def looks(n, parts):
            look[n] = keep.tile([P, M], F32, name="look", tag="look%d" % n, align_bytes=64)
            plain[n] = keep.tile([P, M], F32, name="plain", tag="plain%d" % n, align_bytes=64)
            width = M // parts
            for m in range(0, M, width):
                window = h_t[n][:].indirect(offs2_t[:, m // 16 : (m + width) // 16])
                nc.scalar.activation(out=plain[n][:, m : m + width], in_=window, func=ACT.Copy)
            for m in range(0, M, width):
                window = h_t[n][:].indirect(offs2_t[:, m // 16 : (m + width) // 16])
                nc.scalar.activation(out=look[n][:, m : m + width], in_=window, func=ACT.Exp, bias=minus_top[n][:])

        def place_marked(first, count, slot):
            held = keep.tile([P, count, M], F32, name="marked", tag=slot, align_bytes=64)
            for k in range(count):
                marked[first + k] = held[:, k, :]

        def mark_look(n, engine, cols=slice(0, M)):
            b, i = divmod(n, 4)
            engine.tensor_tensor(out=marked[n][:, cols], in0=mark_z[b][:, i, cols], in1=look[n][:, cols], op=ALU.mult)

        def make_z(n, cols=slice(0, M)):
            b, i = divmod(n, 4)
            nc.vector.scalar_tensor_tensor(
                out=mark_z[b][:, i, cols],
                in0=plain[n][:, cols],
                scalar=gain_col[n],
                in1=marked[n][:, cols],
                op0=ALU.mult,
                op1=ALU.add,
            )

        def interleave(engine, rows):
            unit = rounded.tile([P, 4 * HALF], BF16, name="rounded", tag="rounded", align_bytes=64)
            dst = unit[:].rearrange("p (c i t) -> p c t i", i=4, t=4)
            round_copy(engine, dst, rows.rearrange("p t (c i) -> p c t i", i=4))
            return unit

        def half(c):
            return slice(HALF * c, HALF * (c + 1))

        def quantise_z(b, c):
            nc.vector.quantize_mx(out=z_codes[b][c][:].bitcast(E4M3), scales=z_scales[b][c][:], in_=z_bf16[b, c][:])

        def second_product(b, c):
            for t in range(4):
                if b == 0:
                    y_bank[t, c] = psum.tile([P, HALF], F32, name="bank", tag="bank%d" % (2 * t + c))
                cols = slice(N * b + P * t, N * b + P * (t + 1))
                nc.tensor.matmul_mx(
                    out=y_bank[t, c][:],
                    lhsT=w4_dealt[:, cols].bitcast(E2M1),
                    lhsT_scale=w4s_dealt[:, cols],
                    rhs=z_codes[b][c][:].bitcast(E4M3),
                    rhs_scale=z_scales[b][c][:],
                    start=(b == 0),
                    stop=(b == 1),
                )

        def hand_out(c, y):
            for t in range(4):
                if t % 2 == 0:
                    nc.vector.tensor_copy(out=y[:, t, :], in_=y_bank[t, c][:])
                else:
                    nc.scalar.copy(out=y[:, t, :], in_=y_bank[t, c][:])
            nc.sync.dma_start(out=out_0.rearrange("(p t) m -> p t m", t=4)[:, :, half(c)], in_=y)
            y_bf16 = interleave("vector", y)
            nc.vector.quantize_mx(out=y_codes[:, half(c)].bitcast(E4M3), scales=y_scales[:, half(c)], in_=y_bf16[:])
            nc.sync.dma_start(
                out=out_1[0].rearrange("p m t -> p (m t)").bitcast(I32)[:, half(c)], in_=y_codes[:, half(c)].bitcast(I32)
            )

        nc.gpsimd.memset(tab_s[:].bitcast(I32), 0)
        nc.gpsimd.memset(w4s_raw[:].bitcast(I32), 0)
        for q in range(4):
            nc.gpsimd.dma_start(
                out=w4s_raw[32 * q : 32 * q + 4, :].bitcast(I32).rearrange("r (b c) -> r b c", b=2),
                in_=w4_scales[:, 4 * q : 4 * q + 4, :].bitcast(I32).rearrange("b r c -> r b c"),
            )
        load_tab(0)
        nc.sync.dma_start(out=offs_t[:], in_=offs)
        load_w1(0, 0)
        for q in range(4):
            nc.sync.dma_start(
                out=tab_s[32 * q : 32 * q + 4 * K_PASSES, :].bitcast(I32),
                in_=tab_scales[:, 4 * q : 4 * q + 4, :].bitcast(I32),
            )
        for a in range(1, K_PASSES):
            load_tab(a)
            load_w1(0, a)
        load_hall(0)
        nc.sync.dma_start(out=offs2_t[:], in_=offs2)
        nc.sync.dma_start(out=w4_raw[:].bitcast(I32), in_=w4_words.bitcast(I32).rearrange("b p c -> p b c"))
        load_hall(1)
        load_w1(1, 0)

        for a in range(K_PASSES):
            last = a == K_PASSES - 1
            for c in range(2):
                nc.vector.tensor_copy(out=v_words[a][c][:], in_=tab_t[a][:].indirect(offs_t[:, 32 * c : 32 * (c + 1)]))
            if a == 0:
                for c in range(2):
                    nc.vector.tensor_copy(out=v_scales[c][:], in_=tab_s[:].indirect(offs_t[:, 32 * c : 32 * (c + 1)]))
            round_w1(0, a, 0, "vector" if last else "scalar")
            round_w1(0, a, 1, "scalar", "head_unit" if last else None)
            for u in range(2):
                quantise_w1(0, a, u, "w1_codes%d%d" % (a, u))
        for n in range(4):
            first_product(n)

        nc.scalar.copy(
            out=w4_dealt[:].rearrange("p (b t q) -> p b t q", b=2, t=4),
            in_=w4_raw[:].rearrange("p b (q t) -> p b t q", t=4),
        )
        for a in range(1, K_PASSES):
            load_hall(1 + a)
            load_w1(1, a)
        load_gain(0, 2, "gain0")
        load_gain(4, 4, "gain4")
        w4s_dealt = keep.tile([P, 2 * N], U8, name="w4s_dealt", tag="head_unit", align_bytes=64)
        nc.gpsimd.tensor_copy(
            out=w4s_dealt[:].rearrange("p (b t q) -> p b t q", b=2, t=4),
            in_=w4s_raw[:].rearrange("p (b q t) -> p b t q", b=2, t=4),
        )
        for a in range(2):
            for u in range(2):
                round_w1(1, a, u, "gpsimd")

        for n in range(4):
            make_h(n)
            make_top(n)
            looks(n, 1)

        quantise_wide()
        round_w1(1, 2, 0, "scalar")
        round_w1(1, 2, 1, "scalar", "last_unit")
        load_mark(0, 0, 2)
        load_hall(4)
        load_mark(0, 2, 2)
        for n in range(5, ROW_TILES):
            load_hall(n)
        load_mark(1, 0, 4)
        place_marked(0, 2, "wide")
        for n in range(2):
            mark_look(n, nc.vector)
        quantise_w1(1, 2, 0, "look0")
        for n in range(2):
            make_z(n)
        quantise_w1(1, 2, 1, "plain1")
        place_marked(2, 2, "last_unit")
        for n in range(2, 4):
            mark_look(n, nc.gpsimd)

        first_product(4)
        make_h(4)
        make_top(4)
        looks(4, 1)
        load_gain(2, 2, "hall4")

        first_product(5)
        make_h(5)
        make_top(5)
        looks(5, 1)
        for n in range(2, 4):
            make_z(n)
        for c in range(2):
            z_bf16[0, c] = interleave("scalar", mark_z[0][:, :, half(c)])
        place_marked(4, 1, "plain3")
        mark_look(4, nc.gpsimd)

        first_product(6)
        make_h(6)
        place_marked(5, 1, "hall6")
        mark_look(5, nc.vector)
        make_top(6)
        looks(6, 1)

        first_product(7)
        make_h(7)
        make_top(7)
        looks(7, 2)

        for c in range(2):
            quantise_z(0, c)
            second_product(0, c)
        for n in range(4, 6):
            make_z(n)
        for n in range(6, ROW_TILES):
            marked[n] = mark_z[1][:, n - 4, :]
        mark_look(6, nc.vector)
        for c in range(2):
            mark_look(7, nc.vector, half(c))
        make_z(6)
        for c in range(2):
            make_z(7, half(c))
        for c in range(2):
            z_bf16[1, c] = interleave("vector" if c == 0 else "scalar", mark_z[1][:, :, half(c)])
            quantise_z(1, c)
        y_halves = keep.tile([P, 2, 4, HALF], F32, name="y_halves", tag="w1_slot0", align_bytes=64)
        for c in range(2):
            second_product(1, c)
            hand_out(c, y_halves[:, c])
        for q in range(4):
            queue = nc.sync if q % 2 == 0 else nc.scalar
            queue.dma_start(
                out=out_2[0, 4 * q : 4 * q + 4, :].bitcast(I32), in_=y_scales[32 * q : 32 * q + 4, :].bitcast(I32)
            )
